import numpy as np
import ml_dtypes


def mxq(x, axis, fmt="e4m3"):
    dtype, down = {"e4m3": (ml_dtypes.float8_e4m3fn, 7), "e5m2": (ml_dtypes.float8_e5m2, 14)}[fmt]
    v = np.moveaxis(np.asarray(x, np.float32).astype(ml_dtypes.bfloat16).astype(np.float64), axis, -1)
    blocks = v.reshape(v.shape[:-1] + (-1, 32))
    amax = np.abs(blocks).max(-1, keepdims=True)
    byte = np.maximum(np.where(amax > 0, np.frexp(amax)[1] - 1 + 127, 0) - down, 1)
    scale = np.exp2(byte - 127.0)
    codes = (blocks / scale).astype(np.float32).astype(dtype).astype(np.float64)
    return np.moveaxis((codes * scale).reshape(v.shape), -1, axis)


WIDE = False


def mx_kscale(k):
    if not WIDE:
        return np.ones(k)
    levels = np.array([10, -10, 5, -5, 0])
    if k % 512:
        return np.exp2(np.random.permutation(np.resize(levels, k // 32))).repeat(32)
    a = np.empty((k // 512, 16))
    for p in range(k // 512):
        a[p, :8] = np.random.permutation(np.resize(levels, 8))
        for g in range(8):
            far = levels[np.abs(levels - a[p, g]) >= 10]
            a[p, g + 8] = far[np.random.randint(len(far))]
    return np.exp2(a.ravel()).repeat(32)


BF16 = ml_dtypes.bfloat16


def bf(x):
    return np.asarray(x, np.float32).astype(BF16)


def f64(x):
    return np.asarray(x).astype(np.float64)

def planes(Y):
    n, m = Y.shape
    b = f64(bf(Y)).reshape(n // 32, 32, m)
    amax = np.abs(b).max(1)
    byte = np.clip(np.where(amax > 0, np.frexp(amax)[1] - 1 + 127 - 7, 1), 1, 254)
    codes = (b * np.exp2(127.0 - byte)[:, None, :]).reshape(n, m).astype(np.float32).astype(ml_dtypes.float8_e4m3fn).view(np.uint8)
    words = codes.reshape(n // 512, 128, 4, m).transpose(0, 1, 3, 2)
    return np.ascontiguousarray(words), np.ascontiguousarray(byte.astype(np.uint8).reshape(n // 512, 16, m))


R, S, K, F, Q = 8, 512, 512, 1024, 256
SLOPE = 0.2

def setup_inputs():
    s = mx_kscale(K)
    t = mx_kscale(S)
    spread = np.exp(0.8 * np.random.randn(F))
    x = bf(np.sqrt(2.0) * np.sin(2.0 * np.pi * np.random.rand(R, S, K)) * s)
    w = bf(np.random.randn(K, F) * spread * np.sqrt(2.0 / K) / s[:, None])
    g = bf(np.exp(0.3 * np.random.randn(R, S)) * t)
    v = bf(np.random.randn(Q, S) / np.sqrt(S) / t)
    c = bf(0.5 * np.random.randn(F) * spread)
    return {"x": x, "w": w, "g": g, "v": v, "c": c}

def reference(x, w, g, v, c):
    x, w, g, v, c = f64(x), f64(w), f64(g), f64(v), f64(c)
    a = mxq(x.reshape(R * S, K), 1, "e4m3") @ mxq(w, 0, "e4m3")
    h = np.maximum(a, 0.0).reshape(R, S, F) * g.reshape(R, S, 1)
    z = (mxq(v, 1, "e4m3") @ mxq(h, 1, "e4m3")) + c
    y = np.maximum(z, SLOPE * z)
    Y = y.reshape(R * Q, F).T
    words, scales = planes(Y)
    return y, words, scales

@@ -1,0 +1,312 @@
+from contextlib import ExitStack
+
+import concourse.mybir as mybir
+from concourse.masks import make_identity
+
+R, S, K, F, Q = 8, 512, 512, 1024, 256
+SLOPE = 0.2
+FLOPS = 2 * R * S * K * F + 2 * R * Q * S * F
+
+F32 = mybir.dt.float32
+BF16 = mybir.dt.bfloat16
+I32 = mybir.dt.int32
+U32 = mybir.dt.uint32
+U8 = mybir.dt.uint8
+FP8X4 = mybir.dt.float8_e4m3fn_x4
+ALU = mybir.AluOpType
+ACT = mybir.ActivationFunctionType
+
+P = 128
+PACK = 4
+GROUP = P * PACK
+GROUPS = F // GROUP
+STEPS = R * GROUPS
+
+
+def tile_ray_sample_depth_mixing_h3_kernel(tc, x, w, g, v, c, out_0, out_1, out_2):
+    nc = tc.nc
+    words_out = out_1.rearrange("g p m t -> g p (m t)").bitcast(I32)
+    scales_out = out_2.bitcast(I32)
+
+    with ExitStack() as ctx:
+        keep = ctx.enter_context(tc.tile_pool(name="keep", bufs=1))
+        work = ctx.enter_context(tc.tile_pool(name="work", bufs=2))
+        psum = ctx.enter_context(tc.psum_pool(name="psum", bufs=1))
+        ctx.enter_context(tc.manual_schedule())
+
+        def bank(tag, bufs):
+            return psum.tile([P, GROUP], F32, name=tag, tag=tag, bufs=bufs)
+
+        def a_bank():
+            return bank("a_bank", 3)
+
+        def z_bank():
+            return bank("z_bank", 2)
+
+        def y_bank():
+            return bank("y_bank", 2)
+
+        def x_bank():
+            return bank("x_bank", 1)
+
+        ident = keep.tile([P, P], F32, name="ident")
+        make_identity(nc, ident[:])
+        rows = keep.tile([P, S], BF16, name="rows")
+        nc.vector.memset(rows[:].bitcast(I32), 0)
+
+        x_raw = [keep.tile([P, PACK, K], BF16, name="x_raw%d" % r) for r in range(R)]
+        w_raw = [keep.tile([P, PACK, GROUP], BF16, name="w_raw%d" % j) for j in range(GROUPS)]
+        v_raw = keep.tile([P, 2, S], BF16, name="v_raw")
+
+        def load_x(r):
+            nc.sync.dma_start(out=x_raw[r][:], in_=x[r].rearrange("(m t) k -> m t k", t=PACK))
+
+        load_x(0)
+        nc.sync.dma_start(out=rows[0:R, :], in_=g)
+        nc.sync.dma_start(out=rows[R : R + GROUPS, :], in_=c.rearrange("(j f) -> j f", j=GROUPS))
+        for j in range(GROUPS):
+            nc.sync.dma_start(
+                out=w_raw[j][:],
+                in_=w[:, j * GROUP : (j + 1) * GROUP].rearrange("(p t) f -> p t f", t=PACK),
+            )
+        nc.sync.dma_start(out=v_raw[:], in_=v.rearrange("(a p) s -> p a s", p=P))
+        for r in range(1, R):
+            load_x(r)
+
+        def turn(dst, sources):
+            for i, src in enumerate(sources):
+                pairs = src.bitcast(F32)
+                for u in range(2):
+                    col = (2 * i + u) * P
+                    nc.tensor.transpose(dst[:, col : col + P], pairs[:, u : 2 * P : 2], ident[:])
+
+        def quantize(codes, scales, grouped):
+            nc.vector.quantize_mx(out=codes.bitcast(FP8X4), scales=scales, in_=grouped)
+
+        def mx_tiles(pool, name, width, bufs):
+            codes = pool.tile([P, width], U32, name=name + "_codes", bufs=bufs, align_bytes=64)
+            scales = pool.tile([P, width], U8, name=name + "_scales", bufs=bufs, align_bytes=64)
+            return codes, scales
+
+        x_grouped, x_mx, x_turned = {}, {}, {}
+        a_banks, h_grouped, h_mx, z_banks, small, y_cols, y_grouped = {}, {}, {}, {}, {}, {}, {}
+
+        def turn_x(i, dst):
+            r, half = divmod(i, 2)
+            x_turned[i] = dst
+            turn(dst, [x_raw[r][:, 2 * half + t, :] for t in range(2)])
+
+        def unpack(dst_words, src):
+            nc.scalar.copy(
+                out=dst_words.rearrange("p (s m u) -> p s m u", s=2, u=2),
+                in_=src.rearrange("p (s u m) -> p s m u", s=2, u=2),
+            )
+
+        def copy_x(i):
+            r, half = divmod(i, 2)
+            if half == 0:
+                x_grouped[r] = work.tile([P, S * PACK], BF16, name="x_grouped", align_bytes=64)
+            unpack(x_grouped[r][:].bitcast(F32)[:, half * GROUP : (half + 1) * GROUP], x_turned[i][:])
+
+        def quantize_x(r):
+            x_mx[r] = mx_tiles(work, "x", S, 2)
+            quantize(x_mx[r][0][:], x_mx[r][1][:], x_grouped[r][:])
+
+        w_grouped = [keep.tile([P, GROUP * PACK], BF16, name="w_grouped%d" % j, align_bytes=64) for j in range(GROUPS)]
+        w_mx = [mx_tiles(keep, "w%d" % j, GROUP, 1) for j in range(GROUPS)]
+
+        def group_w(j, copy):
+            copy(
+                out=w_grouped[j][:].rearrange("p (t n i k) -> p n t i k", t=PACK, i=2, k=PACK),
+                in_=w_raw[j][:].rearrange("p k (n i t) -> p n t i k", t=PACK, i=2),
+            )
+
+        def quantize_w(j):
+            quantize(w_mx[j][0][:], w_mx[j][1][:], w_grouped[j][:])
+
+        def layer1(s, n):
+            r, j = divmod(s, GROUPS)
+            dst = a_bank()
+            a_banks[s, n] = dst
+            cols = slice(n * P, (n + 1) * P)
+            for t in range(PACK):
+                slot = slice(t * P, (t + 1) * P)
+                nc.tensor.matmul_mx(
+                    out=dst[:, slot],
+                    lhsT=x_mx[r][0][:, slot].bitcast(FP8X4),
+                    lhsT_scale=x_mx[r][1][:, slot],
+                    rhs=w_mx[j][0][:, cols].bitcast(FP8X4),
+                    rhs_scale=w_mx[j][1][:, cols],
+                    start=True,
+                    stop=True,
+                )
+
+        def make_h(s, n):
+            r = s // GROUPS
+            if n == 0:
+                h_grouped[s] = work.tile([P, GROUP, PACK], BF16, name="h_grouped", align_bytes=64)
+            nc.vector.scalar_tensor_tensor(
+                out=h_grouped[s][:, n * P : (n + 1) * P, :],
+                in0=a_banks[s, n][:].rearrange("p (t f) -> p f t", t=PACK),
+                scalar=0.0,
+                in1=per_slot[:, r, :].unsqueeze(1).to_broadcast([P, P, PACK]),
+                op0=ALU.max,
+                op1=ALU.mult,
+            )
+
+        def quantize_h(s):
+            h_mx[s] = mx_tiles(work, "h", GROUP, 2)
+            quantize(h_mx[s][0][:], h_mx[s][1][:], h_grouped[s][:].rearrange("p f t -> p (f t)"))
+
+        def z_of(s, t):
+            return z_banks[s, t // 2][:, (t % 2) * Q : (t % 2 + 1) * Q]
+
+        def layer2(s):
+            for t in range(PACK):
+                if t % 2 == 0:
+                    z_banks[s, t // 2] = z_bank()
+                slot = slice(t * P, (t + 1) * P)
+                nc.tensor.matmul_mx(
+                    out=z_of(s, t),
+                    lhsT=h_mx[s][0][:, slot].bitcast(FP8X4),
+                    lhsT_scale=h_mx[s][1][:, slot],
+                    rhs=v_mx[0][:].bitcast(FP8X4),
+                    rhs_scale=v_mx[1][:],
+                    start=True,
+                    stop=True,
+                )
+
+        def sloped(s):
+            j = s % GROUPS
+            small[s] = work.tile([P, PACK, Q], F32, name="sloped")
+            for t in range(PACK):
+                nc.scalar.activation(
+                    out=small[s][:, t, :], in_=z_of(s, t), func=ACT.Identity, scale=SLOPE, bias=c_sloped[:, j, t : t + 1]
+                )
+
+        def make_y(s):
+            j = s % GROUPS
+            y_cols[s] = work.tile([P, PACK, Q], F32, name="y_cols", bufs=3)
+            for t in range(PACK):
+                nc.vector.scalar_tensor_tensor(
+                    out=y_cols[s][:, t, :],
+                    in0=z_of(s, t),
+                    scalar=per_slot[:, R + j, t : t + 1],
+                    in1=small[s][:, t, :],
+                    op0=ALU.add,
+                    op1=ALU.max,
+                )
+
+        def group_y(s):
+            y_grouped[s] = work.tile([P, Q * PACK], BF16, name="y_grouped", align_bytes=64)
+            nc.scalar.copy(
+                out=y_grouped[s][:].rearrange("p (b i t) -> p b t i", i=4, t=PACK),
+                in_=y_cols[s][:].rearrange("p t (b i) -> p b t i", i=4),
+            )
+
+        y_scales = keep.tile([P, R * Q], U8, name="y_scales", align_bytes=64)
+
+        def quantize_y(s):
+            r, j = divmod(s, GROUPS)
+            cols = slice(r * Q, (r + 1) * Q)
+            codes = work.tile([P, Q], U32, name="y_codes", bufs=4, align_bytes=64)
+            quantize(codes[:], y_scales[4 * j : P, cols], y_grouped[s][:])
+            nc.sync.dma_start(out=words_out[j, :, cols], in_=codes[:].bitcast(I32))
+
+        y_banks = {}
+
+        def turn_y(s):
+            for a in range(2):
+                dst = y_bank()
+                y_banks[s, a] = dst
+                for t in range(PACK):
+                    nc.tensor.transpose(dst[:, t * P : (t + 1) * P], y_cols[s][:, t, a * P : (a + 1) * P], ident[:])
+
+        def store_y(s):
+            r, j = divmod(s, GROUPS)
+            y_rows = work.tile([P, 2, GROUP], F32, name="y_rows", bufs=4)
+            for a in range(2):
+                nc.scalar.copy(
+                    out=y_rows[:, a, :].rearrange("b (p t) -> b p t", t=PACK),
+                    in_=y_banks[s, a][:].rearrange("b (t p) -> b p t", t=PACK),
+                )
+            nc.sync.dma_start(
+                out=out_0[r, :, j * GROUP : (j + 1) * GROUP].rearrange("(a b) f -> b a f", b=P), in_=y_rows[:]
+            )
+
+        turn_x(0, y_bank())
+        turn_x(1, y_bank())
+        rows_turned = x_bank()
+        turn(rows_turned, [rows[:]])
+        v_turned = z_bank()
+        turn(v_turned, [v_raw[:, a, :] for a in range(2)])
+        copy_x(0)
+        copy_x(1)
+        live = R + GROUPS
+        slot_words = keep.tile([P, live * 2], F32, name="slot_words")
+        nc.scalar.copy(
+            out=slot_words[:].rearrange("p (r u) -> p r u", u=2),
+            in_=rows_turned[:, 0 : 2 * P].rearrange("p (u r) -> p r u", u=2)[:, 0:live, :],
+        )
+        per_slot = slot_words[:].bitcast(BF16).rearrange("p (r t) -> p r t", t=PACK)
+        c_sloped = keep.tile([P, GROUPS, PACK], F32, name="c_sloped")
+        group_w(0, nc.vector.tensor_copy)
+        quantize_w(0)
+        quantize_x(0)
+        layer1(0, 0)
+        group_w(1, nc.scalar.copy)
+        nc.scalar.activation(out=c_sloped[:], in_=per_slot[:, R:live, :], func=ACT.Identity, scale=SLOPE)
+        v_grouped = keep.tile([P, Q * PACK], BF16, name="v_grouped", align_bytes=64)
+        unpack(v_grouped[:].bitcast(F32), v_turned[:])
+        v_mx = mx_tiles(keep, "v", Q, 1)
+        turn_x(2, x_bank())
+        copy_x(2)
+
+        def live_step(s):
+            return 0 <= s < STEPS
+
+        for s in range(STEPS + 3):
+            if live_step(s):
+                layer1(s, 1)
+                layer1(s, 2)
+                make_h(s, 0)
+                layer1(s, 3)
+            if live_step(s - 1):
+                quantize_h(s - 1)
+            if live_step(s):
+                make_h(s, 1)
+            if s == 0:
+                quantize_w(1)
+                quantize(v_mx[0][:], v_mx[1][:], v_grouped[:])
+            if live_step(s - 2):
+                make_y(s - 2)
+            if s % 2 == 1 and live_step(s + 1):
+                quantize_x((s + 1) // 2)
+            if live_step(s - 1):
+                layer2(s - 1)
+            if live_step(s + 1):
+                layer1(s + 1, 0)
+            if live_step(s - 2):
+                group_y(s - 2)
+            if live_step(s - 1):
+                sloped(s - 1)
+            if live_step(s):
+                make_h(s, 2)
+            if live_step(s - 3):
+                quantize_y(s - 3)
+            if live_step(s):
+                make_h(s, 3)
+            if live_step(s + 3):
+                turn_x(s + 3, x_bank())
+            if live_step(s - 2):
+                turn_y(s - 2)
+            if live_step(s + 3):
+                copy_x(s + 3)
+            if live_step(s - 2):
+                store_y(s - 2)
+
+        for quad in range(4):
+            nc.sync.dma_start(
+                out=scales_out[:, 4 * quad : 4 * quad + 4, :],
+                in_=y_scales[32 * quad : 32 * quad + 4 * GROUPS, :].bitcast(I32),
+            )

@@ -21,6 +21,8 @@ PACK = 4
 GROUP = P * PACK
 GROUPS = F // GROUP
 STEPS = R * GROUPS
+W_PART = 256
+POOL_BINS = 176
 
 
 def tile_ray_sample_depth_mixing_h3_kernel(tc, x, w, g, v, c, out_0, out_1, out_2):
@@ -52,26 +54,39 @@ def tile_ray_sample_depth_mixing_h3_kernel(tc, x, w, g, v, c, out_0, out_1, out_
         ident = keep.tile([P, P], F32, name="ident")
         make_identity(nc, ident[:])
         rows = keep.tile([P, S], BF16, name="rows")
-        nc.vector.memset(rows[:].bitcast(I32), 0)
+        nc.scalar.activation(
+            out=rows[:].bitcast(F32).rearrange("p (a b) -> p a b", a=2),
+            in_=ident[:].unsqueeze(1).to_broadcast([P, 2, P]),
+            func=ACT.Identity,
+            scale=0.0,
+        )
 
-        x_raw = [keep.tile([P, PACK, K], BF16, name="x_raw%d" % r) for r in range(R)]
-        w_raw = [keep.tile([P, PACK, GROUP], BF16, name="w_raw%d" % j) for j in range(GROUPS)]
+        x_raw = [keep.tile([P, 2, K], BF16, name="x_raw%d" % i) for i in range(2 * R)]
+        w_raw = [keep.tile([P, PACK, W_PART], BF16, name="w_raw%d" % i) for i in range(F // W_PART)]
         v_raw = keep.tile([P, 2, S], BF16, name="v_raw")
 
-        def load_x(r):
-            nc.sync.dma_start(out=x_raw[r][:], in_=x[r].rearrange("(m t) k -> m t k", t=PACK))
+        def load_x(i):
+            r, half = divmod(i, 2)
+            nc.sync.dma_start(
+                out=x_raw[i][:], in_=x[r].rearrange("(m t) k -> m t k", t=PACK)[:, 2 * half : 2 * half + 2, :]
+            )
+
+        def load_w(i):
+            nc.sync.dma_start(
+                out=w_raw[i][:], in_=w[:, i * W_PART : (i + 1) * W_PART].rearrange("(p t) f -> p t f", t=PACK)
+            )
 
         load_x(0)
+        load_x(1)
+        load_w(0)
+        load_w(1)
         nc.sync.dma_start(out=rows[0:R, :], in_=g)
         nc.sync.dma_start(out=rows[R : R + GROUPS, :], in_=c.rearrange("(j f) -> j f", j=GROUPS))
-        for j in range(GROUPS):
-            nc.sync.dma_start(
-                out=w_raw[j][:],
-                in_=w[:, j * GROUP : (j + 1) * GROUP].rearrange("(p t) f -> p t f", t=PACK),
-            )
+        load_w(2)
+        load_w(3)
         nc.sync.dma_start(out=v_raw[:], in_=v.rearrange("(a p) s -> p a s", p=P))
-        for r in range(1, R):
-            load_x(r)
+        for i in range(2, 2 * R):
+            load_x(i)
 
         def turn(dst, sources):
             for i, src in enumerate(sources):
@@ -92,9 +107,8 @@ def tile_ray_sample_depth_mixing_h3_kernel(tc, x, w, g, v, c, out_0, out_1, out_
         a_banks, h_grouped, h_mx, z_banks, small, y_cols, y_grouped = {}, {}, {}, {}, {}, {}, {}
 
         def turn_x(i, dst):
-            r, half = divmod(i, 2)
             x_turned[i] = dst
-            turn(dst, [x_raw[r][:, 2 * half + t, :] for t in range(2)])
+            turn(dst, [x_raw[i][:, t, :] for t in range(2)])
 
         def unpack(dst_words, src):
             nc.scalar.copy(
@@ -108,17 +122,19 @@ def tile_ray_sample_depth_mixing_h3_kernel(tc, x, w, g, v, c, out_0, out_1, out_
                 x_grouped[r] = work.tile([P, S * PACK], BF16, name="x_grouped", align_bytes=64)
             unpack(x_grouped[r][:].bitcast(F32)[:, half * GROUP : (half + 1) * GROUP], x_turned[i][:])
 
-        def quantize_x(r):
-            x_mx[r] = mx_tiles(work, "x", S, 2)
-            quantize(x_mx[r][0][:], x_mx[r][1][:], x_grouped[r][:])
+        def quantize_x(r, lo=0, hi=S):
+            if lo == 0:
+                x_mx[r] = mx_tiles(work, "x", S, 2)
+            quantize(x_mx[r][0][:, lo:hi], x_mx[r][1][:, lo:hi], x_grouped[r][:, lo * PACK : hi * PACK])
 
         w_grouped = [keep.tile([P, GROUP * PACK], BF16, name="w_grouped%d" % j, align_bytes=64) for j in range(GROUPS)]
         w_mx = [mx_tiles(keep, "w%d" % j, GROUP, 1) for j in range(GROUPS)]
 
-        def group_w(j, copy):
+        def group_w(i, copy):
+            j, half = divmod(i, 2)
             copy(
-                out=w_grouped[j][:].rearrange("p (t n i k) -> p n t i k", t=PACK, i=2, k=PACK),
-                in_=w_raw[j][:].rearrange("p k (n i t) -> p n t i k", t=PACK, i=2),
+                out=w_grouped[j][:].rearrange("p (t h n i k) -> p h n t i k", t=PACK, h=2, i=2, k=PACK)[:, half],
+                in_=w_raw[i][:].rearrange("p k (n i t) -> p n t i k", t=PACK, i=2),
             )
 
         def quantize_w(j):
@@ -144,7 +160,7 @@ def tile_ray_sample_depth_mixing_h3_kernel(tc, x, w, g, v, c, out_0, out_1, out_
         def make_h(s, n):
             r = s // GROUPS
             if n == 0:
-                h_grouped[s] = work.tile([P, GROUP, PACK], BF16, name="h_grouped", align_bytes=64)
+                h_grouped[s] = work.tile([P, GROUP, PACK], BF16, name="h_grouped", bufs=1, align_bytes=64)
             nc.vector.scalar_tensor_tensor(
                 out=h_grouped[s][:, n * P : (n + 1) * P, :],
                 in0=a_banks[s, n][:].rearrange("p (t f) -> p f t", t=PACK),
@@ -154,17 +170,35 @@ def tile_ray_sample_depth_mixing_h3_kernel(tc, x, w, g, v, c, out_0, out_1, out_
                 op1=ALU.mult,
             )
 
-        def quantize_h(s):
-            h_mx[s] = mx_tiles(work, "h", GROUP, 2)
-            quantize(h_mx[s][0][:], h_mx[s][1][:], h_grouped[s][:].rearrange("p f t -> p (f t)"))
+        relu_a = {}
+
+        def relu_first(s):
+            relu_a[s] = work.tile([P, P, PACK], F32, name="relu_a")
+            nc.scalar.activation(
+                out=relu_a[s][:], in_=a_banks[s, 0][:].rearrange("p (t f) -> p f t", t=PACK), func=ACT.Relu
+            )
+
+        def weigh_first(s):
+            h_grouped[s] = work.tile([P, GROUP, PACK], BF16, name="h_grouped", bufs=1, align_bytes=64)
+            nc.gpsimd.tensor_tensor(
+                out=h_grouped[s][:, 0:P, :],
+                in0=relu_a[s][:],
+                in1=per_slot[:, s // GROUPS, :].unsqueeze(1).to_broadcast([P, P, PACK]),
+                op=ALU.mult,
+            )
+
+        def quantize_h(s, lo=0, hi=GROUP):
+            if lo == 0:
+                h_mx[s] = mx_tiles(work, "h", GROUP, 2)
+            quantize(h_mx[s][0][:, lo:hi], h_mx[s][1][:, lo:hi], h_grouped[s][:, lo:hi, :].rearrange("p f t -> p (f t)"))
 
         def z_of(s, t):
             return z_banks[s, t // 2][:, (t % 2) * Q : (t % 2 + 1) * Q]
 
-        def layer2(s):
-            for t in range(PACK):
+        def layer2(s, slots=range(PACK), new_bank=z_bank):
+            for t in slots:
                 if t % 2 == 0:
-                    z_banks[s, t // 2] = z_bank()
+                    z_banks[s, t // 2] = new_bank()
                 slot = slice(t * P, (t + 1) * P)
                 nc.tensor.matmul_mx(
                     out=z_of(s, t),
@@ -176,18 +210,20 @@ def tile_ray_sample_depth_mixing_h3_kernel(tc, x, w, g, v, c, out_0, out_1, out_
                     stop=True,
                 )
 
-        def sloped(s):
+        def sloped(s, slots=range(PACK)):
             j = s % GROUPS
-            small[s] = work.tile([P, PACK, Q], F32, name="sloped")
-            for t in range(PACK):
+            if slots[0] == 0:
+                small[s] = work.tile([P, PACK, Q], F32, name="sloped")
+            for t in slots:
                 nc.scalar.activation(
                     out=small[s][:, t, :], in_=z_of(s, t), func=ACT.Identity, scale=SLOPE, bias=c_sloped[:, j, t : t + 1]
                 )
 
-        def make_y(s):
+        def make_y(s, slots=range(PACK)):
             j = s % GROUPS
-            y_cols[s] = work.tile([P, PACK, Q], F32, name="y_cols", bufs=3)
-            for t in range(PACK):
+            if slots[0] == 0:
+                y_cols[s] = work.tile([P, PACK, Q], F32, name="y_cols", bufs=3)
+            for t in slots:
                 nc.vector.scalar_tensor_tensor(
                     out=y_cols[s][:, t, :],
                     in0=z_of(s, t),
@@ -199,10 +235,23 @@ def tile_ray_sample_depth_mixing_h3_kernel(tc, x, w, g, v, c, out_0, out_1, out_
 
         def group_y(s):
             y_grouped[s] = work.tile([P, Q * PACK], BF16, name="y_grouped", align_bytes=64)
-            nc.scalar.copy(
-                out=y_grouped[s][:].rearrange("p (b i t) -> p b t i", i=4, t=PACK),
-                in_=y_cols[s][:].rearrange("p t (b i) -> p b t i", i=4),
-            )
+
+            def sides(lo, hi):
+                return (
+                    y_grouped[s][:, lo * PACK : hi * PACK].rearrange("p (b i t) -> p b t i", i=4, t=PACK),
+                    y_cols[s][:, :, lo:hi].rearrange("p t (b i) -> p b t i", i=4),
+                )
+
+            if s == STEPS - 1:
+                dst, src = sides(0, Q)
+                nc.vector.tensor_copy(out=dst, in_=src)
+                return
+            split = Q if s == STEPS - 2 else POOL_BINS
+            dst, src = sides(0, split)
+            nc.gpsimd.tensor_scalar(out=dst, in0=src, scalar1=1.0, scalar2=0.0, op0=ALU.mult, op1=ALU.add)
+            if split < Q:
+                dst, src = sides(split, Q)
+                nc.scalar.copy(out=dst, in_=src)
 
         y_scales = keep.tile([P, R * Q], U8, name="y_scales", align_bytes=64)
 
@@ -215,31 +264,37 @@ def tile_ray_sample_depth_mixing_h3_kernel(tc, x, w, g, v, c, out_0, out_1, out_
 
         y_banks = {}
 
-        def turn_y(s):
-            for a in range(2):
-                dst = y_bank()
+        def turn_y(s, halves=range(2), new_bank=y_bank):
+            for a in halves:
+                dst = new_bank()
                 y_banks[s, a] = dst
                 for t in range(PACK):
                     nc.tensor.transpose(dst[:, t * P : (t + 1) * P], y_cols[s][:, t, a * P : (a + 1) * P], ident[:])
 
-        def store_y(s):
+        def store_y(s, halves=range(2), copy=nc.scalar.copy):
             r, j = divmod(s, GROUPS)
-            y_rows = work.tile([P, 2, GROUP], F32, name="y_rows", bufs=4)
-            for a in range(2):
-                nc.scalar.copy(
-                    out=y_rows[:, a, :].rearrange("b (p t) -> b p t", t=PACK),
+            y_rows = work.tile([P, len(halves), GROUP], F32, name="y_rows", bufs=4)
+            for i, a in enumerate(halves):
+                copy(
+                    out=y_rows[:, i, :].rearrange("b (p t) -> b p t", t=PACK),
                     in_=y_banks[s, a][:].rearrange("b (t p) -> b p t", t=PACK),
                 )
+            bins = slice(halves[0] * P, (halves[-1] + 1) * P)
             nc.sync.dma_start(
-                out=out_0[r, :, j * GROUP : (j + 1) * GROUP].rearrange("(a b) f -> b a f", b=P), in_=y_rows[:]
+                out=out_0[r, bins, j * GROUP : (j + 1) * GROUP].rearrange("(a b) f -> b a f", b=P), in_=y_rows[:]
             )
+
+        def store_scales(lo, hi):
+            for quad in range(4):
+                nc.sync.dma_start(
+                    out=scales_out[:, 4 * quad : 4 * quad + 4, lo // 4 : hi // 4],
+                    in_=y_scales[32 * quad : 32 * quad + 4 * GROUPS, lo:hi].bitcast(I32),
+                )
 
         turn_x(0, y_bank())
         turn_x(1, y_bank())
         rows_turned = x_bank()
         turn(rows_turned, [rows[:]])
-        v_turned = z_bank()
-        turn(v_turned, [v_raw[:, a, :] for a in range(2)])
         copy_x(0)
         copy_x(1)
         live = R + GROUPS
@@ -251,62 +306,92 @@ def tile_ray_sample_depth_mixing_h3_kernel(tc, x, w, g, v, c, out_0, out_1, out_
         per_slot = slot_words[:].bitcast(BF16).rearrange("p (r t) -> p r t", t=PACK)
         c_sloped = keep.tile([P, GROUPS, PACK], F32, name="c_sloped")
         group_w(0, nc.vector.tensor_copy)
+        group_w(1, nc.vector.tensor_copy)
+        quantize_x(0, 0, S // 2)
         quantize_w(0)
-        quantize_x(0)
+        quantize_x(0, S // 2, S)
         layer1(0, 0)
-        group_w(1, nc.scalar.copy)
+        group_w(2, nc.scalar.copy)
+        group_w(3, nc.vector.tensor_copy)
         nc.scalar.activation(out=c_sloped[:], in_=per_slot[:, R:live, :], func=ACT.Identity, scale=SLOPE)
         v_grouped = keep.tile([P, Q * PACK], BF16, name="v_grouped", align_bytes=64)
-        unpack(v_grouped[:].bitcast(F32), v_turned[:])
         v_mx = mx_tiles(keep, "v", Q, 1)
-        turn_x(2, x_bank())
-        copy_x(2)
 
         def live_step(s):
             return 0 <= s < STEPS
 
-        for s in range(STEPS + 3):
-            if live_step(s):
-                layer1(s, 1)
-                layer1(s, 2)
+        for s in range(STEPS):
+            layer1(s, 1)
+            layer1(s, 2)
+            if s < 2:
                 make_h(s, 0)
-                layer1(s, 3)
-            if live_step(s - 1):
-                quantize_h(s - 1)
-            if live_step(s):
-                make_h(s, 1)
+            layer1(s, 3)
             if s == 0:
-                quantize_w(1)
-                quantize(v_mx[0][:], v_mx[1][:], v_grouped[:])
-            if live_step(s - 2):
-                make_y(s - 2)
-            if s % 2 == 1 and live_step(s + 1):
-                quantize_x((s + 1) // 2)
-            if live_step(s - 1):
-                layer2(s - 1)
-            if live_step(s + 1):
-                layer1(s + 1, 0)
-            if live_step(s - 2):
-                group_y(s - 2)
-            if live_step(s - 1):
-                sloped(s - 1)
-            if live_step(s):
-                make_h(s, 2)
-            if live_step(s - 3):
-                quantize_y(s - 3)
-            if live_step(s):
-                make_h(s, 3)
-            if live_step(s + 3):
-                turn_x(s + 3, x_bank())
-            if live_step(s - 2):
-                turn_y(s - 2)
+                v_turned = z_bank()
+                turn(v_turned, [v_raw[:, a, :] for a in range(2)])
+                unpack(v_grouped[:].bitcast(F32), v_turned[:])
+                turn_x(2, y_bank())
+                turn_x(3, y_bank())
+                copy_x(2)
             if live_step(s + 3):
                 copy_x(s + 3)
+            if live_step(s - 3):
+                store_y(s - 3)
+            if s % 2 == 1 and live_step(s + 1) and s > 1:
+                quantize_x((s + 1) // 2)
+            if live_step(s - 3):
+                quantize_y(s - 3)
+            if s >= 2:
+                if s > 2:
+                    quantize_h(s - 1)
+                weigh_first(s)
             if live_step(s - 2):
-                store_y(s - 2)
+                make_y(s - 2)
+                group_y(s - 2)
+            if live_step(s - 1):
+                layer2(s - 1)
+                sloped(s - 1)
+            make_h(s, 1)
+            if s == 0:
+                quantize_w(1)
+            if s == 1:
+                quantize_x(1)
+            if live_step(s + 1):
+                layer1(s + 1, 0)
+                if s + 1 >= 2:
+                    relu_first(s + 1)
+            make_h(s, 2)
+            if s == STEPS - 1:
+                quantize_h(s, 0, GROUP // 2)
+                layer2(s, range(0, 2), x_bank)
+            make_h(s, 3)
+            if s == 0:
+                quantize(v_mx[0][:], v_mx[1][:], v_grouped[:])
+            if s < 2:
+                quantize_h(s)
+            if live_step(s + 4):
+                turn_x(s + 4, x_bank())
+            if live_step(s - 2):
+                turn_y(s - 2)
 
-        for quad in range(4):
-            nc.sync.dma_start(
-                out=scales_out[:, 4 * quad : 4 * quad + 4, :],
-                in_=y_scales[32 * quad : 32 * quad + 4 * GROUPS, :].bitcast(I32),
-            )
+        last = STEPS - 1
+        quantize_y(last - 2)
+        store_scales(0, (R - 1) * Q)
+        quantize_h(last, GROUP // 2, GROUP)
+        layer2(last, range(2, 4), a_bank)
+        sloped(last, range(0, 2))
+        store_y(last - 2, range(0, 1))
+        make_y(last - 1)
+        group_y(last - 1)
+        sloped(last, range(2, 4))
+        store_y(last - 2, range(1, 2))
+        turn_y(last - 1)
+        make_y(last)
+        store_y(last - 1)
+        turn_y(last, range(2), a_bank)
+        group_y(last)
+        quantize_y(last - 1)
+        store_y(last, range(0, 1))
+        quantize_y(last)
+        store_y(last, range(1, 2), nc.vector.tensor_copy)
+        store_scales((R - 1) * Q, R * Q)

@@ -21,8 +21,7 @@ PACK = 4
 GROUP = P * PACK
 GROUPS = F // GROUP
 STEPS = R * GROUPS
-W_PART = 256
-POOL_BINS = 176
+POOL_BINS = 160
 
 
 def tile_ray_sample_depth_mixing_h3_kernel(tc, x, w, g, v, c, out_0, out_1, out_2):
@@ -36,20 +35,23 @@ def tile_ray_sample_depth_mixing_h3_kernel(tc, x, w, g, v, c, out_0, out_1, out_
         psum = ctx.enter_context(tc.psum_pool(name="psum", bufs=1))
         ctx.enter_context(tc.manual_schedule())
 
-        def bank(tag, bufs):
-            return psum.tile([P, GROUP], F32, name=tag, tag=tag, bufs=bufs)
-
         def a_bank():
-            return bank("a_bank", 3)
+            return psum.tile([P, GROUP], F32, name="a_bank", bufs=3)
 
         def z_bank():
-            return bank("z_bank", 2)
+            return psum.tile([P, GROUP], F32, name="z_bank", bufs=2)
 
         def y_bank():
-            return bank("y_bank", 2)
+            return psum.tile([P, GROUP], F32, name="y_bank", bufs=2)
 
         def x_bank():
-            return bank("x_bank", 1)
+            return psum.tile([P, GROUP], F32, name="x_bank", bufs=1)
+
+        def ray_of(s):
+            return s // GROUPS
+
+        def group_of(s):
+            return s % GROUPS
 
         ident = keep.tile([P, P], F32, name="ident")
         make_identity(nc, ident[:])
@@ -62,7 +64,7 @@ def tile_ray_sample_depth_mixing_h3_kernel(tc, x, w, g, v, c, out_0, out_1, out_
         )
 
         x_raw = [keep.tile([P, 2, K], BF16, name="x_raw%d" % i) for i in range(2 * R)]
-        w_raw = [keep.tile([P, PACK, W_PART], BF16, name="w_raw%d" % i) for i in range(F // W_PART)]
+        w_raw = [keep.tile([P, PACK, GROUP], BF16, name="w_raw%d" % j) for j in range(GROUPS)]
         v_raw = keep.tile([P, 2, S], BF16, name="v_raw")
 
         def load_x(i):
@@ -71,19 +73,17 @@ def tile_ray_sample_depth_mixing_h3_kernel(tc, x, w, g, v, c, out_0, out_1, out_
                 out=x_raw[i][:], in_=x[r].rearrange("(m t) k -> m t k", t=PACK)[:, 2 * half : 2 * half + 2, :]
             )
 
-        def load_w(i):
+        def load_w(j):
             nc.sync.dma_start(
-                out=w_raw[i][:], in_=w[:, i * W_PART : (i + 1) * W_PART].rearrange("(p t) f -> p t f", t=PACK)
+                out=w_raw[j][:], in_=w[:, j * GROUP : (j + 1) * GROUP].rearrange("(p t) f -> p t f", t=PACK)
             )
 
         load_x(0)
         load_x(1)
         load_w(0)
-        load_w(1)
         nc.sync.dma_start(out=rows[0:R, :], in_=g)
         nc.sync.dma_start(out=rows[R : R + GROUPS, :], in_=c.rearrange("(j f) -> j f", j=GROUPS))
-        load_w(2)
-        load_w(3)
+        load_w(1)
         nc.sync.dma_start(out=v_raw[:], in_=v.rearrange("(a p) s -> p a s", p=P))
         for i in range(2, 2 * R):
             load_x(i)
@@ -95,6 +95,12 @@ def tile_ray_sample_depth_mixing_h3_kernel(tc, x, w, g, v, c, out_0, out_1, out_
                     col = (2 * i + u) * P
                     nc.tensor.transpose(dst[:, col : col + P], pairs[:, u : 2 * P : 2], ident[:])
 
+        def unpack(dst_words, src, copy=nc.scalar.copy):
+            copy(
+                out=dst_words.rearrange("p (i m u) -> p i m u", i=2, u=2),
+                in_=src.rearrange("p (i u m) -> p i m u", i=2, u=2),
+            )
+
         def quantize(codes, scales, grouped):
             nc.vector.quantize_mx(out=codes.bitcast(FP8X4), scales=scales, in_=grouped)
 
@@ -103,24 +109,30 @@ def tile_ray_sample_depth_mixing_h3_kernel(tc, x, w, g, v, c, out_0, out_1, out_
             scales = pool.tile([P, width], U8, name=name + "_scales", bufs=bufs, align_bytes=64)
             return codes, scales
 
-        x_grouped, x_mx, x_turned = {}, {}, {}
-        a_banks, h_grouped, h_mx, z_banks, small, y_cols, y_grouped = {}, {}, {}, {}, {}, {}, {}
-
-        def turn_x(i, dst):
-            x_turned[i] = dst
-            turn(dst, [x_raw[i][:, t, :] for t in range(2)])
-
-        def unpack(dst_words, src):
-            nc.scalar.copy(
-                out=dst_words.rearrange("p (s m u) -> p s m u", s=2, u=2),
-                in_=src.rearrange("p (s u m) -> p s m u", s=2, u=2),
+        def multiply(dst, lhs, lhs_cols, rhs, rhs_cols):
+            nc.tensor.matmul_mx(
+                out=dst,
+                lhsT=lhs[0][:, lhs_cols].bitcast(FP8X4),
+                lhsT_scale=lhs[1][:, lhs_cols],
+                rhs=rhs[0][:, rhs_cols].bitcast(FP8X4),
+                rhs_scale=rhs[1][:, rhs_cols],
+                start=True,
+                stop=True,
             )
 
-        def copy_x(i):
+        x_turned, x_grouped, x_mx = {}, {}, {}
+        a_banks, relu_a, h_grouped, h_mx = {}, {}, {}, {}
+        z_banks, sloped, y_cols, y_grouped, y_banks = {}, {}, {}, {}, {}
+
+        def turn_x(i, new_bank=x_bank):
+            x_turned[i] = new_bank()
+            turn(x_turned[i], [x_raw[i][:, t, :] for t in range(2)])
+
+        def copy_x(i, copy=nc.scalar.copy):
             r, half = divmod(i, 2)
             if half == 0:
                 x_grouped[r] = work.tile([P, S * PACK], BF16, name="x_grouped", align_bytes=64)
-            unpack(x_grouped[r][:].bitcast(F32)[:, half * GROUP : (half + 1) * GROUP], x_turned[i][:])
+            unpack(x_grouped[r][:].bitcast(F32)[:, half * GROUP : (half + 1) * GROUP], x_turned[i][:], copy)
 
         def quantize_x(r, lo=0, hi=S):
             if lo == 0:
@@ -130,62 +142,48 @@ def tile_ray_sample_depth_mixing_h3_kernel(tc, x, w, g, v, c, out_0, out_1, out_
         w_grouped = [keep.tile([P, GROUP * PACK], BF16, name="w_grouped%d" % j, align_bytes=64) for j in range(GROUPS)]
         w_mx = [mx_tiles(keep, "w%d" % j, GROUP, 1) for j in range(GROUPS)]
 
-        def group_w(i, copy):
-            j, half = divmod(i, 2)
+        def group_w(j, lo, hi, copy):
             copy(
-                out=w_grouped[j][:].rearrange("p (t h n i k) -> p h n t i k", t=PACK, h=2, i=2, k=PACK)[:, half],
-                in_=w_raw[i][:].rearrange("p k (n i t) -> p n t i k", t=PACK, i=2),
+                out=w_grouped[j][:].rearrange("p (t n i k) -> p n t i k", t=PACK, i=2, k=PACK)[:, :, lo:hi],
+                in_=w_raw[j][:].rearrange("p k (n i t) -> p n t i k", t=PACK, i=2)[:, :, lo:hi],
             )
 
-        def quantize_w(j):
-            quantize(w_mx[j][0][:], w_mx[j][1][:], w_grouped[j][:])
+        def quantize_w(j, lo=0, hi=PACK):
+            cols = slice(lo * P, hi * P)
+            quantize(w_mx[j][0][:, cols], w_mx[j][1][:, cols], w_grouped[j][:, lo * GROUP : hi * GROUP])
 
         def layer1(s, n):
-            r, j = divmod(s, GROUPS)
-            dst = a_bank()
-            a_banks[s, n] = dst
-            cols = slice(n * P, (n + 1) * P)
+            a_banks[s, n] = a_bank()
             for t in range(PACK):
                 slot = slice(t * P, (t + 1) * P)
-                nc.tensor.matmul_mx(
-                    out=dst[:, slot],
-                    lhsT=x_mx[r][0][:, slot].bitcast(FP8X4),
-                    lhsT_scale=x_mx[r][1][:, slot],
-                    rhs=w_mx[j][0][:, cols].bitcast(FP8X4),
-                    rhs_scale=w_mx[j][1][:, cols],
-                    start=True,
-                    stop=True,
-                )
+                multiply(a_banks[s, n][:, slot], x_mx[ray_of(s)], slot, w_mx[group_of(s)], slice(n * P, (n + 1) * P))
+
+        def g_of(s):
+            return per_slot[:, ray_of(s), :].unsqueeze(1).to_broadcast([P, P, PACK])
+
+        def h_part(s, n):
+            if s not in h_grouped:
+                h_grouped[s] = work.tile([P, GROUP, PACK], BF16, name="h_grouped", bufs=1, align_bytes=64)
+            return h_grouped[s][:, n * P : (n + 1) * P, :]
 
         def make_h(s, n):
-            r = s // GROUPS
-            if n == 0:
-                h_grouped[s] = work.tile([P, GROUP, PACK], BF16, name="h_grouped", bufs=1, align_bytes=64)
             nc.vector.scalar_tensor_tensor(
-                out=h_grouped[s][:, n * P : (n + 1) * P, :],
+                out=h_part(s, n),
                 in0=a_banks[s, n][:].rearrange("p (t f) -> p f t", t=PACK),
                 scalar=0.0,
-                in1=per_slot[:, r, :].unsqueeze(1).to_broadcast([P, P, PACK]),
+                in1=g_of(s),
                 op0=ALU.max,
                 op1=ALU.mult,
             )
 
-        relu_a = {}
-
-        def relu_first(s):
-            relu_a[s] = work.tile([P, P, PACK], F32, name="relu_a")
+        def relu(s, n):
+            relu_a[s, n] = work.tile([P, P, PACK], F32, name="relu_a")
             nc.scalar.activation(
-                out=relu_a[s][:], in_=a_banks[s, 0][:].rearrange("p (t f) -> p f t", t=PACK), func=ACT.Relu
+                out=relu_a[s, n][:], in_=a_banks[s, n][:].rearrange("p (t f) -> p f t", t=PACK), func=ACT.Relu
             )
 
-        def weigh_first(s):
-            h_grouped[s] = work.tile([P, GROUP, PACK], BF16, name="h_grouped", bufs=1, align_bytes=64)
-            nc.gpsimd.tensor_tensor(
-                out=h_grouped[s][:, 0:P, :],
-                in0=relu_a[s][:],
-                in1=per_slot[:, s // GROUPS, :].unsqueeze(1).to_broadcast([P, P, PACK]),
-                op=ALU.mult,
-            )
+        def weigh(s, n):
+            nc.gpsimd.tensor_tensor(out=h_part(s, n), in0=relu_a[s, n][:], in1=g_of(s), op=ALU.mult)
 
         def quantize_h(s, lo=0, hi=GROUP):
             if lo == 0:
@@ -199,80 +197,63 @@ def tile_ray_sample_depth_mixing_h3_kernel(tc, x, w, g, v, c, out_0, out_1, out_
             for t in slots:
                 if t % 2 == 0:
                     z_banks[s, t // 2] = new_bank()
-                slot = slice(t * P, (t + 1) * P)
-                nc.tensor.matmul_mx(
-                    out=z_of(s, t),
-                    lhsT=h_mx[s][0][:, slot].bitcast(FP8X4),
-                    lhsT_scale=h_mx[s][1][:, slot],
-                    rhs=v_mx[0][:].bitcast(FP8X4),
-                    rhs_scale=v_mx[1][:],
-                    start=True,
-                    stop=True,
-                )
+                multiply(z_of(s, t), h_mx[s], slice(t * P, (t + 1) * P), v_mx, slice(0, Q))
 
-        def sloped(s, slots=range(PACK)):
-            j = s % GROUPS
+        def slope(s, slots=range(PACK)):
             if slots[0] == 0:
-                small[s] = work.tile([P, PACK, Q], F32, name="sloped")
+                sloped[s] = work.tile([P, PACK, Q], F32, name="sloped")
             for t in slots:
                 nc.scalar.activation(
-                    out=small[s][:, t, :], in_=z_of(s, t), func=ACT.Identity, scale=SLOPE, bias=c_sloped[:, j, t : t + 1]
+                    out=sloped[s][:, t, :],
+                    in_=z_of(s, t),
+                    func=ACT.Identity,
+                    scale=SLOPE,
+                    bias=c_sloped[:, group_of(s), t : t + 1],
                 )
 
         def make_y(s, slots=range(PACK)):
-            j = s % GROUPS
             if slots[0] == 0:
                 y_cols[s] = work.tile([P, PACK, Q], F32, name="y_cols", bufs=3)
             for t in slots:
                 nc.vector.scalar_tensor_tensor(
                     out=y_cols[s][:, t, :],
                     in0=z_of(s, t),
-                    scalar=per_slot[:, R + j, t : t + 1],
-                    in1=small[s][:, t, :],
+                    scalar=per_slot[:, R + group_of(s), t : t + 1],
+                    in1=sloped[s][:, t, :],
                     op0=ALU.add,
                     op1=ALU.max,
                 )
 
-        def group_y(s):
-            y_grouped[s] = work.tile([P, Q * PACK], BF16, name="y_grouped", align_bytes=64)
+        def pool_copy(out, in_):
+            nc.gpsimd.tensor_scalar(out=out, in0=in_, scalar1=1.0, scalar2=0.0, op0=ALU.mult, op1=ALU.add)
 
-            def sides(lo, hi):
-                return (
-                    y_grouped[s][:, lo * PACK : hi * PACK].rearrange("p (b i t) -> p b t i", i=4, t=PACK),
-                    y_cols[s][:, :, lo:hi].rearrange("p t (b i) -> p b t i", i=4),
-                )
-
-            if s == STEPS - 1:
-                dst, src = sides(0, Q)
-                nc.vector.tensor_copy(out=dst, in_=src)
-                return
-            split = Q if s == STEPS - 2 else POOL_BINS
-            dst, src = sides(0, split)
-            nc.gpsimd.tensor_scalar(out=dst, in0=src, scalar1=1.0, scalar2=0.0, op0=ALU.mult, op1=ALU.add)
-            if split < Q:
-                dst, src = sides(split, Q)
-                nc.scalar.copy(out=dst, in_=src)
+        def group_y(s, lo, hi, copy):
+            if s not in y_grouped:
+                y_grouped[s] = work.tile([P, Q * PACK], BF16, name="y_grouped", align_bytes=64)
+            copy(
+                out=y_grouped[s][:, lo * PACK : hi * PACK].rearrange("p (b i t) -> p b t i", i=4, t=PACK),
+                in_=y_cols[s][:, :, lo:hi].rearrange("p t (b i) -> p b t i", i=4),
+            )
 
         y_scales = keep.tile([P, R * Q], U8, name="y_scales", align_bytes=64)
 
         def quantize_y(s):
-            r, j = divmod(s, GROUPS)
-            cols = slice(r * Q, (r + 1) * Q)
+            cols = slice(ray_of(s) * Q, (ray_of(s) + 1) * Q)
             codes = work.tile([P, Q], U32, name="y_codes", bufs=4, align_bytes=64)
-            quantize(codes[:], y_scales[4 * j : P, cols], y_grouped[s][:])
-            nc.sync.dma_start(out=words_out[j, :, cols], in_=codes[:].bitcast(I32))
+            quantize(codes[:], y_scales[4 * group_of(s) : P, cols], y_grouped[s][:])
+            nc.sync.dma_start(out=words_out[group_of(s), :, cols], in_=codes[:].bitcast(I32))
 
-        y_banks = {}
-
-        def turn_y(s, halves=range(2), new_bank=y_bank):
+        def turn_y(s, halves=range(2), new_bank=y_bank, slots=range(PACK)):
             for a in halves:
-                dst = new_bank()
-                y_banks[s, a] = dst
-                for t in range(PACK):
-                    nc.tensor.transpose(dst[:, t * P : (t + 1) * P], y_cols[s][:, t, a * P : (a + 1) * P], ident[:])
+                if slots[0] == 0:
+                    y_banks[s, a] = new_bank()
+                for t in slots:
+                    nc.tensor.transpose(
+                        y_banks[s, a][:, t * P : (t + 1) * P], y_cols[s][:, t, a * P : (a + 1) * P], ident[:]
+                    )
 
         def store_y(s, halves=range(2), copy=nc.scalar.copy):
-            r, j = divmod(s, GROUPS)
+            j = group_of(s)
             y_rows = work.tile([P, len(halves), GROUP], F32, name="y_rows", bufs=4)
             for i, a in enumerate(halves):
                 copy(
@@ -281,7 +262,7 @@ def tile_ray_sample_depth_mixing_h3_kernel(tc, x, w, g, v, c, out_0, out_1, out_
                 )
             bins = slice(halves[0] * P, (halves[-1] + 1) * P)
             nc.sync.dma_start(
-                out=out_0[r, bins, j * GROUP : (j + 1) * GROUP].rearrange("(a b) f -> b a f", b=P), in_=y_rows[:]
+                out=out_0[ray_of(s), bins, j * GROUP : (j + 1) * GROUP].rearrange("(a b) f -> b a f", b=P), in_=y_rows[:]
             )
 
         def store_scales(lo, hi):
@@ -291,8 +272,8 @@ def tile_ray_sample_depth_mixing_h3_kernel(tc, x, w, g, v, c, out_0, out_1, out_
                     in_=y_scales[32 * quad : 32 * quad + 4 * GROUPS, lo:hi].bitcast(I32),
                 )
 
-        turn_x(0, y_bank())
-        turn_x(1, y_bank())
+        turn_x(0, y_bank)
+        turn_x(1, y_bank)
         rows_turned = x_bank()
         turn(rows_turned, [rows[:]])
         copy_x(0)
@@ -305,93 +286,125 @@ def tile_ray_sample_depth_mixing_h3_kernel(tc, x, w, g, v, c, out_0, out_1, out_
         )
         per_slot = slot_words[:].bitcast(BF16).rearrange("p (r t) -> p r t", t=PACK)
         c_sloped = keep.tile([P, GROUPS, PACK], F32, name="c_sloped")
-        group_w(0, nc.vector.tensor_copy)
-        group_w(1, nc.vector.tensor_copy)
-        quantize_x(0, 0, S // 2)
-        quantize_w(0)
-        quantize_x(0, S // 2, S)
-        layer1(0, 0)
-        group_w(2, nc.scalar.copy)
-        group_w(3, nc.vector.tensor_copy)
-        nc.scalar.activation(out=c_sloped[:], in_=per_slot[:, R:live, :], func=ACT.Identity, scale=SLOPE)
         v_grouped = keep.tile([P, Q * PACK], BF16, name="v_grouped", align_bytes=64)
         v_mx = mx_tiles(keep, "v", Q, 1)
+        group_w(0, 0, 2, nc.vector.tensor_copy)
+        quantize_x(0, 0, S // 2)
+        quantize_w(0, 0, 2)
+        quantize_x(0, S // 2, S)
+        layer1(0, 0)
+        layer1(0, 1)
+        group_w(0, 2, 4, nc.vector.tensor_copy)
+        group_w(1, 0, 2, nc.scalar.copy)
+        group_w(1, 2, 4, nc.scalar.copy)
+        v_turned = z_bank()
+        turn(v_turned, [v_raw[:, a, :] for a in range(2)])
+        quantize_w(0, 2, 4)
+        make_h(0, 0)
+        layer1(0, 2)
+        layer1(0, 3)
+        make_h(0, 1)
+        quantize_w(1, 0, 2)
+        layer1(1, 0)
+        unpack(v_grouped[:].bitcast(F32), v_turned[:])
+        relu(1, 0)
+        turn_x(2, y_bank)
+        turn_x(3, y_bank)
+        make_h(0, 2)
+        quantize_w(1, 2, 4)
+        make_h(0, 3)
+        copy_x(2)
+        copy_x(3)
+        nc.scalar.activation(out=c_sloped[:], in_=per_slot[:, R:live, :], func=ACT.Identity, scale=SLOPE)
+        layer1(1, 1)
+        layer1(1, 2)
+        layer1(1, 3)
+        quantize(v_mx[0][:], v_mx[1][:], v_grouped[:])
+        quantize_h(0)
+        weigh(1, 0)
+        layer2(0)
+        slope(0)
+        make_h(1, 1)
+        make_h(1, 2)
+        quantize_x(1)
+        layer1(2, 0)
+        relu(2, 0)
+        make_h(1, 3)
+        turn_x(4, y_bank)
+        turn_x(5)
+        copy_x(4)
 
-        def live_step(s):
-            return 0 <= s < STEPS
-
-        for s in range(STEPS):
+        for s in range(2, STEPS - 1):
             layer1(s, 1)
             layer1(s, 2)
-            if s < 2:
-                make_h(s, 0)
             layer1(s, 3)
-            if s == 0:
-                v_turned = z_bank()
-                turn(v_turned, [v_raw[:, a, :] for a in range(2)])
-                unpack(v_grouped[:].bitcast(F32), v_turned[:])
-                turn_x(2, y_bank())
-                turn_x(3, y_bank())
-                copy_x(2)
-            if live_step(s + 3):
+            if s + 3 < STEPS:
                 copy_x(s + 3)
-            if live_step(s - 3):
+            if s >= 3:
                 store_y(s - 3)
-            if s % 2 == 1 and live_step(s + 1) and s > 1:
+            if s % 2 == 1 and 1 < s < STEPS - 1:
                 quantize_x((s + 1) // 2)
-            if live_step(s - 3):
+            if s >= 3:
                 quantize_y(s - 3)
+            quantize_h(s - 1)
+            weigh(s, 0)
             if s >= 2:
-                if s > 2:
-                    quantize_h(s - 1)
-                weigh_first(s)
-            if live_step(s - 2):
                 make_y(s - 2)
-                group_y(s - 2)
-            if live_step(s - 1):
-                layer2(s - 1)
-                sloped(s - 1)
+                if s < STEPS - 1:
+                    group_y(s - 2, 0, POOL_BINS, pool_copy)
+                    group_y(s - 2, POOL_BINS, Q, nc.scalar.copy)
+            layer2(s - 1)
+            slope(s - 1)
             make_h(s, 1)
-            if s == 0:
-                quantize_w(1)
             if s == 1:
                 quantize_x(1)
-            if live_step(s + 1):
+            if s + 1 < STEPS:
                 layer1(s + 1, 0)
-                if s + 1 >= 2:
-                    relu_first(s + 1)
+                relu(s + 1, 0)
             make_h(s, 2)
-            if s == STEPS - 1:
-                quantize_h(s, 0, GROUP // 2)
-                layer2(s, range(0, 2), x_bank)
             make_h(s, 3)
-            if s == 0:
-                quantize(v_mx[0][:], v_mx[1][:], v_grouped[:])
-            if s < 2:
-                quantize_h(s)
-            if live_step(s + 4):
-                turn_x(s + 4, x_bank())
-            if live_step(s - 2):
+            if s + 4 < STEPS:
+                turn_x(s + 4)
+            if s >= 2:
                 turn_y(s - 2)
 
         last = STEPS - 1
+        layer1(last, 1)
+        layer1(last, 2)
+        layer1(last, 3)
+        store_y(last - 3)
+        quantize_y(last - 3)
+        quantize_h(last - 1)
+        weigh(last, 0)
+        make_y(last - 2)
+        group_y(last - 2, 0, POOL_BINS, pool_copy)
+        group_y(last - 2, POOL_BINS, Q, nc.scalar.copy)
+        layer2(last - 1)
+        slope(last - 1)
+        turn_y(last - 2)
+        make_h(last, 1)
+        make_h(last, 2)
+        store_y(last - 2, range(0, 1))
+        make_h(last, 3)
+        quantize_h(last, 0, GROUP // 2)
+        layer2(last, range(0, 2), x_bank)
         quantize_y(last - 2)
         store_scales(0, (R - 1) * Q)
         quantize_h(last, GROUP // 2, GROUP)
         layer2(last, range(2, 4), a_bank)
-        sloped(last, range(0, 2))
-        store_y(last - 2, range(0, 1))
-        make_y(last - 1)
-        group_y(last - 1)
-        sloped(last, range(2, 4))
         store_y(last - 2, range(1, 2))
-        turn_y(last - 1)
-        make_y(last)
-        store_y(last - 1)
-        turn_y(last, range(2), a_bank)
-        group_y(last)
-        quantize_y(last - 1)
+        slope(last)
+        make_y(last - 1)
+        group_y(last - 1, 0, Q, pool_copy)
+        turn_y(last - 1, range(2), a_bank)
+        for t in range(PACK):
+            make_y(last, range(t, t + 1))
+            turn_y(last, range(2), y_bank, range(t, t + 1))
+        store_y(last - 1, range(0, 1))
+        store_y(last - 1, range(1, 2))
+        group_y(last, 0, Q, nc.vector.tensor_copy)
         store_y(last, range(0, 1))
+        quantize_y(last - 1)
         quantize_y(last)
-        store_y(last, range(1, 2), nc.vector.tensor_copy)
+        store_y(last, range(1, 2))
         store_scales((R - 1) * Q, R * Q)

from contextlib import ExitStack

import concourse.mybir as mybir
from concourse.masks import make_identity

R, S, K, F, Q = 8, 512, 512, 1024, 256
SLOPE = 0.2
FLOPS = 2 * R * S * K * F + 2 * R * Q * S * F

F32 = mybir.dt.float32
BF16 = mybir.dt.bfloat16
I32 = mybir.dt.int32
U32 = mybir.dt.uint32
U8 = mybir.dt.uint8
FP8X4 = mybir.dt.float8_e4m3fn_x4
ALU = mybir.AluOpType
ACT = mybir.ActivationFunctionType

P = 128
PACK = 4
GROUP = P * PACK
GROUPS = F // GROUP
STEPS = R * GROUPS
POOL_BINS = 160


def tile_ray_sample_depth_mixing_h3_kernel(tc, x, w, g, v, c, out_0, out_1, out_2):
    nc = tc.nc
    words_out = out_1.rearrange("g p m t -> g p (m t)").bitcast(I32)
    scales_out = out_2.bitcast(I32)

    with ExitStack() as ctx:
        keep = ctx.enter_context(tc.tile_pool(name="keep", bufs=1))
        work = ctx.enter_context(tc.tile_pool(name="work", bufs=2))
        psum = ctx.enter_context(tc.psum_pool(name="psum", bufs=1))
        ctx.enter_context(tc.manual_schedule())

        def a_bank():
            return psum.tile([P, GROUP], F32, name="a_bank", bufs=3)

        def z_bank():
            return psum.tile([P, GROUP], F32, name="z_bank", bufs=2)

        def y_bank():
            return psum.tile([P, GROUP], F32, name="y_bank", bufs=2)

        def x_bank():
            return psum.tile([P, GROUP], F32, name="x_bank", bufs=1)

        def ray_of(s):
            return s // GROUPS

        def group_of(s):
            return s % GROUPS

        ident = keep.tile([P, P], F32, name="ident")
        make_identity(nc, ident[:])
        rows = keep.tile([P, S], BF16, name="rows")
        nc.scalar.activation(
            out=rows[:].bitcast(F32).rearrange("p (a b) -> p a b", a=2),
            in_=ident[:].unsqueeze(1).to_broadcast([P, 2, P]),
            func=ACT.Identity,
            scale=0.0,
        )

        x_raw = [keep.tile([P, 2, K], BF16, name="x_raw%d" % i) for i in range(2 * R)]
        w_raw = [keep.tile([P, PACK, GROUP], BF16, name="w_raw%d" % j) for j in range(GROUPS)]
        v_raw = keep.tile([P, 2, S], BF16, name="v_raw")

        def load_x(i):
            r, half = divmod(i, 2)
            nc.sync.dma_start(
                out=x_raw[i][:], in_=x[r].rearrange("(m t) k -> m t k", t=PACK)[:, 2 * half : 2 * half + 2, :]
            )

        def load_w(j):
            nc.sync.dma_start(
                out=w_raw[j][:], in_=w[:, j * GROUP : (j + 1) * GROUP].rearrange("(p t) f -> p t f", t=PACK)
            )

        load_x(0)
        load_x(1)
        load_w(0)
        nc.sync.dma_start(out=rows[0:R, :], in_=g)
        nc.sync.dma_start(out=rows[R : R + GROUPS, :], in_=c.rearrange("(j f) -> j f", j=GROUPS))
        load_w(1)
        nc.sync.dma_start(out=v_raw[:], in_=v.rearrange("(a p) s -> p a s", p=P))
        for i in range(2, 2 * R):
            load_x(i)

        def turn(dst, sources):
            for i, src in enumerate(sources):
                pairs = src.bitcast(F32)
                for u in range(2):
                    col = (2 * i + u) * P
                    nc.tensor.transpose(dst[:, col : col + P], pairs[:, u : 2 * P : 2], ident[:])

        def unpack(dst_words, src, copy=nc.scalar.copy):
            copy(
                out=dst_words.rearrange("p (i m u) -> p i m u", i=2, u=2),
                in_=src.rearrange("p (i u m) -> p i m u", i=2, u=2),
            )

        def quantize(codes, scales, grouped):
            nc.vector.quantize_mx(out=codes.bitcast(FP8X4), scales=scales, in_=grouped)

        def mx_tiles(pool, name, width, bufs):
            codes = pool.tile([P, width], U32, name=name + "_codes", bufs=bufs, align_bytes=64)
            scales = pool.tile([P, width], U8, name=name + "_scales", bufs=bufs, align_bytes=64)
            return codes, scales

        def multiply(dst, lhs, lhs_cols, rhs, rhs_cols):
            nc.tensor.matmul_mx(
                out=dst,
                lhsT=lhs[0][:, lhs_cols].bitcast(FP8X4),
                lhsT_scale=lhs[1][:, lhs_cols],
                rhs=rhs[0][:, rhs_cols].bitcast(FP8X4),
                rhs_scale=rhs[1][:, rhs_cols],
                start=True,
                stop=True,
            )

        x_turned, x_grouped, x_mx = {}, {}, {}
        a_banks, relu_a, h_grouped, h_mx = {}, {}, {}, {}
        z_banks, sloped, y_cols, y_grouped, y_banks = {}, {}, {}, {}, {}

        def turn_x(i, new_bank=x_bank):
            x_turned[i] = new_bank()
            turn(x_turned[i], [x_raw[i][:, t, :] for t in range(2)])

        def copy_x(i, copy=nc.scalar.copy):
            r, half = divmod(i, 2)
            if half == 0:
                x_grouped[r] = work.tile([P, S * PACK], BF16, name="x_grouped", align_bytes=64)
            unpack(x_grouped[r][:].bitcast(F32)[:, half * GROUP : (half + 1) * GROUP], x_turned[i][:], copy)

        def quantize_x(r, lo=0, hi=S):
            if lo == 0:
                x_mx[r] = mx_tiles(work, "x", S, 2)
            quantize(x_mx[r][0][:, lo:hi], x_mx[r][1][:, lo:hi], x_grouped[r][:, lo * PACK : hi * PACK])

        w_grouped = [keep.tile([P, GROUP * PACK], BF16, name="w_grouped%d" % j, align_bytes=64) for j in range(GROUPS)]
        w_mx = [mx_tiles(keep, "w%d" % j, GROUP, 1) for j in range(GROUPS)]

        def group_w(j, lo, hi, copy):
            copy(
                out=w_grouped[j][:].rearrange("p (t n i k) -> p n t i k", t=PACK, i=2, k=PACK)[:, :, lo:hi],
                in_=w_raw[j][:].rearrange("p k (n i t) -> p n t i k", t=PACK, i=2)[:, :, lo:hi],
            )

        def quantize_w(j, lo=0, hi=PACK):
            cols = slice(lo * P, hi * P)
            quantize(w_mx[j][0][:, cols], w_mx[j][1][:, cols], w_grouped[j][:, lo * GROUP : hi * GROUP])

        def layer1(s, n):
            a_banks[s, n] = a_bank()
            for t in range(PACK):
                slot = slice(t * P, (t + 1) * P)
                multiply(a_banks[s, n][:, slot], x_mx[ray_of(s)], slot, w_mx[group_of(s)], slice(n * P, (n + 1) * P))

        def g_of(s):
            return per_slot[:, ray_of(s), :].unsqueeze(1).to_broadcast([P, P, PACK])

        def h_part(s, n):
            if s not in h_grouped:
                h_grouped[s] = work.tile([P, GROUP, PACK], BF16, name="h_grouped", bufs=1, align_bytes=64)
            return h_grouped[s][:, n * P : (n + 1) * P, :]

        def make_h(s, n):
            nc.vector.scalar_tensor_tensor(
                out=h_part(s, n),
                in0=a_banks[s, n][:].rearrange("p (t f) -> p f t", t=PACK),
                scalar=0.0,
                in1=g_of(s),
                op0=ALU.max,
                op1=ALU.mult,
            )

        def relu(s, n):
            relu_a[s, n] = work.tile([P, P, PACK], F32, name="relu_a")
            nc.scalar.activation(
                out=relu_a[s, n][:], in_=a_banks[s, n][:].rearrange("p (t f) -> p f t", t=PACK), func=ACT.Relu
            )

        def weigh(s, n):
            nc.gpsimd.tensor_tensor(out=h_part(s, n), in0=relu_a[s, n][:], in1=g_of(s), op=ALU.mult)

        def quantize_h(s, lo=0, hi=GROUP):
            if lo == 0:
                h_mx[s] = mx_tiles(work, "h", GROUP, 2)
            quantize(h_mx[s][0][:, lo:hi], h_mx[s][1][:, lo:hi], h_grouped[s][:, lo:hi, :].rearrange("p f t -> p (f t)"))

        def z_of(s, t):
            return z_banks[s, t // 2][:, (t % 2) * Q : (t % 2 + 1) * Q]

        def layer2(s, slots=range(PACK), new_bank=z_bank):
            for t in slots:
                if t % 2 == 0:
                    z_banks[s, t // 2] = new_bank()
                multiply(z_of(s, t), h_mx[s], slice(t * P, (t + 1) * P), v_mx, slice(0, Q))

        def slope(s, slots=range(PACK)):
            if slots[0] == 0:
                sloped[s] = work.tile([P, PACK, Q], F32, name="sloped")
            for t in slots:
                nc.scalar.activation(
                    out=sloped[s][:, t, :],
                    in_=z_of(s, t),
                    func=ACT.Identity,
                    scale=SLOPE,
                    bias=c_sloped[:, group_of(s), t : t + 1],
                )

        def make_y(s, slots=range(PACK)):
            if slots[0] == 0:
                y_cols[s] = work.tile([P, PACK, Q], F32, name="y_cols", bufs=3)
            for t in slots:
                nc.vector.scalar_tensor_tensor(
                    out=y_cols[s][:, t, :],
                    in0=z_of(s, t),
                    scalar=per_slot[:, R + group_of(s), t : t + 1],
                    in1=sloped[s][:, t, :],
                    op0=ALU.add,
                    op1=ALU.max,
                )

        def pool_copy(out, in_):
            nc.gpsimd.tensor_scalar(out=out, in0=in_, scalar1=1.0, scalar2=0.0, op0=ALU.mult, op1=ALU.add)

        def group_y(s, lo, hi, copy):
            if s not in y_grouped:
                y_grouped[s] = work.tile([P, Q * PACK], BF16, name="y_grouped", align_bytes=64)
            copy(
                out=y_grouped[s][:, lo * PACK : hi * PACK].rearrange("p (b i t) -> p b t i", i=4, t=PACK),
                in_=y_cols[s][:, :, lo:hi].rearrange("p t (b i) -> p b t i", i=4),
            )

        y_scales = keep.tile([P, R * Q], U8, name="y_scales", align_bytes=64)

        def quantize_y(s):
            cols = slice(ray_of(s) * Q, (ray_of(s) + 1) * Q)
            codes = work.tile([P, Q], U32, name="y_codes", bufs=4, align_bytes=64)
            quantize(codes[:], y_scales[4 * group_of(s) : P, cols], y_grouped[s][:])
            nc.sync.dma_start(out=words_out[group_of(s), :, cols], in_=codes[:].bitcast(I32))

        def turn_y(s, halves=range(2), new_bank=y_bank, slots=range(PACK)):
            for a in halves:
                if slots[0] == 0:
                    y_banks[s, a] = new_bank()
                for t in slots:
                    nc.tensor.transpose(
                        y_banks[s, a][:, t * P : (t + 1) * P], y_cols[s][:, t, a * P : (a + 1) * P], ident[:]
                    )

        def store_y(s, halves=range(2), copy=nc.scalar.copy):
            j = group_of(s)
            y_rows = work.tile([P, len(halves), GROUP], F32, name="y_rows", bufs=4)
            for i, a in enumerate(halves):
                copy(
                    out=y_rows[:, i, :].rearrange("b (p t) -> b p t", t=PACK),
                    in_=y_banks[s, a][:].rearrange("b (t p) -> b p t", t=PACK),
                )
            bins = slice(halves[0] * P, (halves[-1] + 1) * P)
            nc.sync.dma_start(
                out=out_0[ray_of(s), bins, j * GROUP : (j + 1) * GROUP].rearrange("(a b) f -> b a f", b=P), in_=y_rows[:]
            )

        def store_scales(lo, hi):
            for quad in range(4):
                nc.sync.dma_start(
                    out=scales_out[:, 4 * quad : 4 * quad + 4, lo // 4 : hi // 4],
                    in_=y_scales[32 * quad : 32 * quad + 4 * GROUPS, lo:hi].bitcast(I32),
                )

        turn_x(0, y_bank)
        turn_x(1, y_bank)
        rows_turned = x_bank()
        turn(rows_turned, [rows[:]])
        copy_x(0)
        copy_x(1)
        live = R + GROUPS
        slot_words = keep.tile([P, live * 2], F32, name="slot_words")
        nc.scalar.copy(
            out=slot_words[:].rearrange("p (r u) -> p r u", u=2),
            in_=rows_turned[:, 0 : 2 * P].rearrange("p (u r) -> p r u", u=2)[:, 0:live, :],
        )
        per_slot = slot_words[:].bitcast(BF16).rearrange("p (r t) -> p r t", t=PACK)
        c_sloped = keep.tile([P, GROUPS, PACK], F32, name="c_sloped")
        v_grouped = keep.tile([P, Q * PACK], BF16, name="v_grouped", align_bytes=64)
        v_mx = mx_tiles(keep, "v", Q, 1)
        group_w(0, 0, 2, nc.vector.tensor_copy)
        quantize_x(0, 0, S // 2)
        quantize_w(0, 0, 2)
        quantize_x(0, S // 2, S)
        layer1(0, 0)
        layer1(0, 1)
        group_w(0, 2, 4, nc.vector.tensor_copy)
        group_w(1, 0, 2, nc.scalar.copy)
        group_w(1, 2, 4, nc.scalar.copy)
        v_turned = z_bank()
        turn(v_turned, [v_raw[:, a, :] for a in range(2)])
        quantize_w(0, 2, 4)
        make_h(0, 0)
        layer1(0, 2)
        layer1(0, 3)
        make_h(0, 1)
        quantize_w(1, 0, 2)
        layer1(1, 0)
        unpack(v_grouped[:].bitcast(F32), v_turned[:])
        relu(1, 0)
        turn_x(2, y_bank)
        turn_x(3, y_bank)
        make_h(0, 2)
        quantize_w(1, 2, 4)
        make_h(0, 3)
        copy_x(2)
        copy_x(3)
        nc.scalar.activation(out=c_sloped[:], in_=per_slot[:, R:live, :], func=ACT.Identity, scale=SLOPE)
        layer1(1, 1)
        layer1(1, 2)
        layer1(1, 3)
        quantize(v_mx[0][:], v_mx[1][:], v_grouped[:])
        quantize_h(0)
        weigh(1, 0)
        layer2(0)
        slope(0)
        make_h(1, 1)
        make_h(1, 2)
        quantize_x(1)
        layer1(2, 0)
        relu(2, 0)
        make_h(1, 3)
        turn_x(4, y_bank)
        turn_x(5)
        copy_x(4)

        for s in range(2, STEPS - 1):
            layer1(s, 1)
            layer1(s, 2)
            layer1(s, 3)
            if s + 3 < STEPS:
                copy_x(s + 3)
            if s >= 3:
                store_y(s - 3)
            if s % 2 == 1 and 1 < s < STEPS - 1:
                quantize_x((s + 1) // 2)
            if s >= 3:
                quantize_y(s - 3)
            quantize_h(s - 1)
            weigh(s, 0)
            if s >= 2:
                make_y(s - 2)
                if s < STEPS - 1:
                    group_y(s - 2, 0, POOL_BINS, pool_copy)
                    group_y(s - 2, POOL_BINS, Q, nc.scalar.copy)
            layer2(s - 1)
            slope(s - 1)
            make_h(s, 1)
            if s == 1:
                quantize_x(1)
            if s + 1 < STEPS:
                layer1(s + 1, 0)
                relu(s + 1, 0)
            make_h(s, 2)
            make_h(s, 3)
            if s + 4 < STEPS:
                turn_x(s + 4)
            if s >= 2:
                turn_y(s - 2)

        last = STEPS - 1
        layer1(last, 1)
        layer1(last, 2)
        layer1(last, 3)
        store_y(last - 3)
        quantize_y(last - 3)
        quantize_h(last - 1)
        weigh(last, 0)
        make_y(last - 2)
        group_y(last - 2, 0, POOL_BINS, pool_copy)
        group_y(last - 2, POOL_BINS, Q, nc.scalar.copy)
        layer2(last - 1)
        slope(last - 1)
        turn_y(last - 2)
        make_h(last, 1)
        make_h(last, 2)
        store_y(last - 2, range(0, 1))
        make_h(last, 3)
        quantize_h(last, 0, GROUP // 2)
        layer2(last, range(0, 2), x_bank)
        quantize_y(last - 2)
        store_scales(0, (R - 1) * Q)
        quantize_h(last, GROUP // 2, GROUP)
        layer2(last, range(2, 4), a_bank)
        store_y(last - 2, range(1, 2))
        slope(last)
        make_y(last - 1)
        group_y(last - 1, 0, Q, pool_copy)
        turn_y(last - 1, range(2), a_bank)
        for t in range(PACK):
            make_y(last, range(t, t + 1))
            turn_y(last, range(2), y_bank, range(t, t + 1))
        store_y(last - 1, range(0, 1))
        store_y(last - 1, range(1, 2))
        group_y(last, 0, Q, nc.vector.tensor_copy)
        store_y(last, range(0, 1))
        quantize_y(last - 1)
        quantize_y(last)
        store_y(last, range(1, 2))
        store_scales((R - 1) * Q, R * Q)
